import numpy as np
import ml_dtypes


def mxq(x, axis, fmt="e4m3"):
    dtype, down = {"e4m3": (ml_dtypes.float8_e4m3fn, 7), "e5m2": (ml_dtypes.float8_e5m2, 14)}[fmt]
    v = np.moveaxis(np.asarray(x, np.float32).astype(ml_dtypes.bfloat16).astype(np.float64), axis, -1)
    blocks = v.reshape(v.shape[:-1] + (-1, 32))
    amax = np.abs(blocks).max(-1, keepdims=True)
    byte = np.maximum(np.where(amax > 0, np.frexp(amax)[1] - 1 + 127, 0) - down, 1)
    scale = np.exp2(byte - 127.0)
    codes = (blocks / scale).astype(np.float32).astype(dtype).astype(np.float64)
    return np.moveaxis((codes * scale).reshape(v.shape), -1, axis)


WIDE = False


def mx_kscale(k):
    if not WIDE:
        return np.ones(k)
    levels = np.array([10, -10, 5, -5, 0])
    if k % 512:
        return np.exp2(np.random.permutation(np.resize(levels, k // 32))).repeat(32)
    a = np.empty((k // 512, 16))
    for p in range(k // 512):
        a[p, :8] = np.random.permutation(np.resize(levels, 8))
        for g in range(8):
            far = levels[np.abs(levels - a[p, g]) >= 10]
            a[p, g + 8] = far[np.random.randint(len(far))]
    return np.exp2(a.ravel()).repeat(32)


def f64(x):
    return np.asarray(x).astype(np.float64)


def striped(idx):
    return np.tile(idx.reshape(-1, 16).T, (8, 1)).astype(np.uint16)


def unstriped(offs):
    return offs[:16].T.reshape(-1).astype(np.int64)


def striped8(idx):
    return np.concatenate([x.reshape(-1, 16).T for x in idx]).astype(np.uint16)


def runs(offs, k):
    lists = np.stack([offs[16 * r : 16 * r + 16].T.reshape(-1) for r in range(8)]).astype(np.int64)
    return lists[np.arange(k) % 512 // 64]


def pack_weight(w):
    k, n = w.shape
    w = f64(np.asarray(w, np.float32).astype(ml_dtypes.bfloat16)).reshape(k // 32, 32, n)
    amax = np.abs(w).max(1)
    byte = np.clip(np.where(amax > 0, np.frexp(amax)[1] - 1 + 127 - 7, 1), 1, 254)
    scaled = (w * np.exp2(127.0 - byte)[:, None, :]).reshape(k, n).astype(np.float32)
    words = np.ascontiguousarray(scaled.reshape(k // 512, 128, 4, n).transpose(0, 1, 3, 2)).astype(ml_dtypes.float8_e4m3fn).view(np.uint8)
    return words, np.ascontiguousarray(byte.astype(np.uint8).reshape(k // 512, 16, n))


def unpack_weight(words, scales):
    g, p, n, _ = words.shape
    vals = np.ascontiguousarray(words).view(ml_dtypes.float8_e4m3fn).astype(np.float64) * np.repeat(np.exp2(scales.astype(np.float64) - 127.0), 8, axis=1)[..., None]
    return vals.transpose(0, 1, 3, 2).reshape(g * 512, n)


def sigmoid(v):
    return 1.0 / (1.0 + np.exp(-np.maximum(v, -700.0)))


K, T, S, N, H, C = 512, 2048, 512, 512, 512, 512


def setup_inputs():
    n = np.random.standard_normal
    s = mx_kscale(K)[:, None]
    u = mx_kscale(S)
    packed_xT = pack_weight(n((K, T)) * s)
    return {
        "x_words": packed_xT[0],
        "x_scales": packed_xT[1],
        "w1": (n((K, H)) / np.sqrt(K) / s).astype(np.float32),
        "sl": np.random.uniform(1.0, 2.0, (H, 1)).astype(np.float32),
        "th": (0.5 * n((H, 1))).astype(np.float32),
        "gn": (np.random.uniform(0.5, 1.5, (H, 1)) * u[:, None]).astype(np.float32),
        "w2": (n((H, N)) / np.sqrt(H) / u[:, None]).astype(np.float32),
        "gs": (np.random.uniform(0.5, 1.5, (K, 1)) / s).astype(np.float32),
        "sl2": np.random.uniform(1.0, 2.0, (N, 1)).astype(np.float32),
        "th2": (0.5 * n((N, 1))).astype(np.float32),
        "sl3": np.random.uniform(1.0, 2.0, (C, 1)).astype(np.float32),
        "th3": (0.5 * n((C, 1))).astype(np.float32),
        "offs": striped(np.random.permutation(T)[:S]),
        "n1": striped8(np.stack([np.random.permutation(S) for _ in range(8)])),
        "n2": striped8(np.stack([np.random.permutation(S) for _ in range(8)])),
        "n3": striped8(np.stack([np.random.permutation(S) for _ in range(8)])),
        "n4": striped8(np.stack([np.random.permutation(S) for _ in range(8)])),
        "cand": striped(np.random.permutation(T)[:C]),
        "n5": striped8(np.stack([np.random.permutation(S) for _ in range(8)])),
        "n6": striped8(np.stack([np.random.permutation(S) for _ in range(8)])),
    }


def reference(x_words, x_scales, w1, sl, th, gn, w2, gs, sl2, th2, sl3, th3, offs, n1, n2, n3, n4, cand, n5, n6):
    xq = unpack_weight(x_words, x_scales)[:, unstriped(offs)]
    y = mxq(f64(w1), 0, "e4m3").T @ xq
    z = f64(gn) * ((y - (y[np.arange(H)[:, None], runs(n1, H)])) * (sigmoid(y[np.arange(H)[:, None], runs(n2, H)])))
    a = mxq(f64(w2), 0, "e4m3").T @ mxq(z, 0, "e4m3")
    sg2 = sigmoid(f64(sl2) * (a[np.arange(N)[:, None], runs(n5, N)] - f64(th2)))
    x_cand = unpack_weight(x_words, x_scales)[:, unstriped(cand)]
    pa = y[np.arange(H)[:, None], runs(n3, H)]
    sg = sigmoid(f64(sl) * (y[np.arange(H)[:, None], runs(n4, H)] - f64(th)))
    z2 = f64(gs) * (pa + sg * (y - pa))
    b = 0.0625 * ((x_cand.T @ mxq(z2, 0, "e4m3")))
    sg3 = sigmoid(f64(sl3) * (b[np.arange(C)[:, None], runs(n6, C)] - f64(th3)))
    return sg2 * b + sg3 * a

@@ -1,0 +1,207 @@
+from contextlib import ExitStack
+
+import concourse.mybir as mybir
+
+F32 = mybir.dt.float32
+BF16 = mybir.dt.bfloat16
+I32 = mybir.dt.int32
+U32 = mybir.dt.uint32
+U16 = mybir.dt.uint16
+U8 = mybir.dt.uint8
+FP8X4 = mybir.dt.float8_e4m3fn_x4
+MULT = mybir.AluOpType.mult
+ADD = mybir.AluOpType.add
+SUB = mybir.AluOpType.subtract
+SIGMOID = mybir.ActivationFunctionType.Sigmoid
+COPY = mybir.ActivationFunctionType.Copy
+
+P = 128
+PACK = 4
+T = 2048
+S = 512
+HALF = S // 2
+FLOPS = 3 * 2 * 512 * 512 * 512
+
+
+def tile_picked_fkcdcxbgdifebl_none_p_kernel(tc, x_words, x_scales, w1, sl, th, gn, w2, gs, sl2, th2, sl3, th3, offs, n1, n2, n3, n4, cand, n5, n6, out):
+    nc = tc.nc
+    with ExitStack() as ctx:
+        pool = ctx.enter_context(tc.tile_pool(name="sbuf", bufs=1))
+        psum = ctx.enter_context(tc.psum_pool(name="psum", bufs=1))
+
+        def load_list(name, src):
+            t = pool.tile([P, S // 16], U16, name=name)
+            nc.sync.dma_start(t[:], src)
+            return t
+
+        def load_rows(name, src):
+            t = pool.tile([P, PACK], F32, name=name)
+            nc.gpsimd.dma_start(t[:], src.rearrange("(p t) o -> p (t o)", t=PACK))
+            return t
+
+        def load_weight_half(name, w, h):
+            t = pool.tile([P, PACK, HALF], F32, name=name)
+            nc.sync.dma_start(t[:], w.rearrange("(p j) c -> p j c", j=PACK)[:, :, h * HALF : (h + 1) * HALF])
+            return t
+
+        def planes(name, width=S):
+            return [pool.tile([P, width], F32, name=f"{name}{t}") for t in range(PACK)]
+
+        xs_all = pool.tile([P, T], U8, name="xs_all")
+        nc.vector.memset(xs_all[:].bitcast(I32), 0)
+        offs_t = load_list("offs_t", offs)
+        cand_t = load_list("cand_t", cand)
+        for q in range(4):
+            nc.sync.dma_start(xs_all[32 * q : 32 * q + 4, :].bitcast(I32), x_scales[0, 4 * q : 4 * q + 4, :].bitcast(I32))
+        xw_all = pool.tile([P, T], I32, name="xw_all")
+        nc.sync.dma_start(xw_all[:], x_words[0].rearrange("p n t -> p (n t)").bitcast(I32))
+        w1_raw = [load_weight_half(f"w1_raw{h}", w1, h) for h in range(2)]
+        n4_t = load_list("n4_t", n4)
+        n3_t = load_list("n3_t", n3)
+        n2_t = load_list("n2_t", n2)
+        n1_t = load_list("n1_t", n1)
+        w2_raw = [load_weight_half(f"w2_raw{h}", w2, h) for h in range(2)]
+        n6_t = load_list("n6_t", n6)
+        n5_t = load_list("n5_t", n5)
+        sl_t = load_rows("sl_t", sl)
+        th_t = load_rows("th_t", th)
+        gs_t = load_rows("gs_t", gs)
+        gn_t = load_rows("gn_t", gn)
+        y_win = planes("y_win", 2 * S)
+        for w in y_win:
+            nc.gpsimd.memset(w[:, S:], 0.0)
+        sl3_t = load_rows("sl3_t", sl3)
+        th3_t = load_rows("th3_t", th3)
+        sl2_t = load_rows("sl2_t", sl2)
+        th2_t = load_rows("th2_t", th2)
+
+        def sigmoid_bias(name, slope, threshold):
+            prod = pool.tile([P, PACK], F32, name=name + "_prod")
+            bias = pool.tile([P, PACK], F32, name=name)
+            nc.gpsimd.tensor_tensor(prod[:], slope[:], threshold[:], MULT)
+            nc.gpsimd.tensor_scalar(bias[:], prod[:], -1.0, 0.0, MULT, ADD)
+            return bias
+
+        bias_y = sigmoid_bias("bias_y", sl_t, th_t)
+        bias_b = sigmoid_bias("bias_b", sl3_t, th3_t)
+        bias_a = sigmoid_bias("bias_a", sl2_t, th2_t)
+
+        b_win = planes("b_win", 2 * S)
+
+        xs = pool.tile([P, S], U8, name="xs", align_bytes=64)
+        xw = pool.tile([P, S], U32, name="xw", align_bytes=64)
+        cs = pool.tile([P, PACK, P], U8, name="cs", align_bytes=64)
+        cw = pool.tile([P, PACK, P], U32, name="cw", align_bytes=64)
+        nc.vector.tensor_copy(xs[:], xs_all[:].indirect(offs_t[:]))
+        nc.vector.tensor_copy(cs[:].rearrange("p t m -> p m t"), xs_all[:].indirect(cand_t[:]))
+        nc.vector.tensor_copy(xw[:], xw_all[:].bitcast(U32).indirect(offs_t[:]))
+        nc.vector.tensor_copy(cw[:].rearrange("p t m -> p m t"), xw_all[:].bitcast(U32).indirect(cand_t[:]))
+
+        def deal_weight_half(copy, grouped, raw, h):
+            m = HALF // PACK
+            copy(
+                grouped[:, :, h * m : (h + 1) * m, :].rearrange("p t m j -> p m j t"),
+                raw[:].rearrange("p j (m t) -> p m j t", t=PACK),
+            )
+
+        def mx_tiles(name):
+            grouped = pool.tile([P, PACK * S], BF16, name=name + "_bf", align_bytes=64)
+            codes = pool.tile([P, S], U32, name=name + "_codes", align_bytes=64)
+            scales = pool.tile([P, S], U8, name=name + "_scales", align_bytes=64)
+            return grouped, codes, scales
+
+        def quantize(mx, lo, hi):
+            grouped, codes, scales = mx
+            nc.vector.quantize_mx(codes[:, lo:hi].bitcast(FP8X4), scales[:, lo:hi], grouped[:, PACK * lo : PACK * hi])
+
+        def product(bank, lhs_codes, lhs_scales, rhs_codes, rhs_scales):
+            nc.tensor.matmul_mx(bank[:], lhsT=lhs_codes.bitcast(FP8X4), lhsT_scale=lhs_scales,
+                                rhs=rhs_codes.bitcast(FP8X4), rhs_scale=rhs_scales, start=True, stop=True)
+
+        def interleave(mx, z):
+            nc.vector.tensor_copy(
+                mx[0][:].rearrange("p (c i t) -> p c t i", i=4, t=PACK),
+                z[:].rearrange("p t (c i) -> p c t i", i=4),
+            )
+
+        def weight_view(mx):
+            return mx[0][:].rearrange("p (t m j) -> p t m j", t=PACK, j=PACK)
+
+        w1_mx = mx_tiles("w1")
+        deal_weight_half(nc.scalar.copy, weight_view(w1_mx), w1_raw[0], 0)
+        deal_weight_half(nc.vector.tensor_copy, weight_view(w1_mx), w1_raw[1], 1)
+        y_ps = [psum.tile([P, S], F32, name=f"y_ps{t}", tag=f"ya{t}") for t in range(PACK)]
+        for t in range(PACK):
+            quantize(w1_mx, t * P, (t + 1) * P)
+            product(y_ps[t], w1_mx[1][:, t * P : (t + 1) * P], w1_mx[2][:, t * P : (t + 1) * P], xw[:], xs[:])
+
+        sg, pa = planes("sg"), planes("pa")
+        e = [w[:, S:] for w in b_win]
+        s2, yn = planes("s2"), planes("yn")
+        z2 = pool.tile([P, PACK, S], F32, name="z2")
+        z = pool.tile([P, PACK, S], F32, name="z")
+
+        def col(v, t):
+            return v[:, t : t + 1]
+
+        for t in range(PACK):
+            if t < 2:
+                nc.vector.tensor_copy(y_win[t][:, :S], y_ps[t][:])
+            else:
+                nc.scalar.copy(y_win[t][:, :S], y_ps[t][:])
+            nc.scalar.activation(sg[t][:], y_win[t][:].indirect(n4_t[:]), SIGMOID, bias=col(bias_y, t), scale=col(sl_t, t))
+        for pair in ((0, 1), (2, 3)):
+            for t in pair:
+                nc.vector.tensor_copy(pa[t][:], y_win[t][:].indirect(n3_t[:]))
+            for t in pair:
+                nc.vector.tensor_tensor(e[t], y_ps[t][:], pa[t][:], SUB)
+            for t in pair:
+                nc.vector.scalar_tensor_tensor(e[t], e[t], col(gs_t, t), sg[t][:], MULT, MULT)
+            for t in pair:
+                nc.vector.scalar_tensor_tensor(z2[:, t, :], pa[t][:], col(gs_t, t), e[t], MULT, ADD)
+        for t in range(PACK):
+            nc.scalar.activation(yn[t][:], y_win[t][:].indirect(n1_t[:]), COPY)
+            nc.scalar.activation(s2[t][:], y_win[t][:].indirect(n2_t[:]), SIGMOID)
+
+        z2_mx = mx_tiles("z2")
+        w2_mx = mx_tiles("w2")
+        interleave(z2_mx, z2)
+        deal_weight_half(nc.vector.tensor_copy, weight_view(w2_mx), w2_raw[0], 0)
+        quantize(z2_mx, 0, S)
+        b_ps = [psum.tile([P, S], F32, name=f"b_ps{t}", tag=f"b{t}") for t in range(PACK)]
+        for t in range(PACK):
+            product(b_ps[t], cw[:, t, :], cs[:, t, :], z2_mx[1][:], z2_mx[2][:])
+        deal_weight_half(nc.vector.tensor_copy, weight_view(w2_mx), w2_raw[1], 1)
+        for t in range(PACK):
+            nc.vector.tensor_tensor(yn[t][:], y_ps[t][:], yn[t][:], SUB)
+        quantize(w2_mx, 0, S)
+        for t in range(PACK):
+            nc.vector.scalar_tensor_tensor(z[:, t, :], yn[t][:], col(gn_t, t), s2[t][:], MULT, MULT)
+
+        sg3, sg2 = planes("sg3"), planes("sg2")
+        for t in range(PACK):
+            nc.scalar.activation(b_win[t][:, :S], b_ps[t][:], COPY, scale=0.0625)
+            nc.scalar.activation(sg3[t][:], b_win[t][:].indirect(n6_t[:]), SIGMOID, bias=col(bias_b, t), scale=col(sl3_t, t))
+
+        z_mx = mx_tiles("z")
+        interleave(z_mx, z)
+        quantize(z_mx, 0, S)
+        a_ps = [psum.tile([P, S], F32, name=f"a_ps{t}", tag=f"ya{t}") for t in range(PACK)]
+        for t in range(PACK):
+            product(a_ps[t], w2_mx[1][:, t * P : (t + 1) * P], w2_mx[2][:, t * P : (t + 1) * P], z_mx[1][:], z_mx[2][:])
+
+        a_win = y_win
+        res = planes("res")
+        out_rows = out.rearrange("(p t) n -> t p n", t=PACK)
+        for t in range(PACK):
+            if t < 3:
+                nc.vector.tensor_copy(a_win[t][:, :S], a_ps[t][:])
+            else:
+                nc.scalar.copy(a_win[t][:, :S], a_ps[t][:])
+            nc.scalar.activation(sg2[t][:], a_win[t][:].indirect(n5_t[:]), SIGMOID, bias=col(bias_a, t), scale=col(sl2_t, t))
+        for t in range(PACK):
+            nc.vector.tensor_tensor(sg3[t][:], a_ps[t][:], sg3[t][:], MULT)
+            nc.vector.scalar_tensor_tensor(sg2[t][:], b_ps[t][:], 0.0625, sg2[t][:], MULT, MULT)
+            adder = nc.gpsimd if t < 3 else nc.vector
+            adder.tensor_tensor(res[t][:], sg2[t][:], sg3[t][:], ADD)
+            nc.sync.dma_start(out_rows[t], res[t][:])

@@ -34,9 +34,9 @@ def tile_picked_fkcdcxbgdifebl_none_p_kernel(tc, x_words, x_scales, w1, sl, th, 
             nc.sync.dma_start(t[:], src)
             return t
 
-        def load_rows(name, src):
+        def load_rows(name, src, queue):
             t = pool.tile([P, PACK], F32, name=name)
-            nc.gpsimd.dma_start(t[:], src.rearrange("(p t) o -> p (t o)", t=PACK))
+            queue.dma_start(t[:], src.rearrange("(p t) o -> p (t o)", t=PACK))
             return t
 
         def load_weight_half(name, w, h):
@@ -48,7 +48,7 @@ def tile_picked_fkcdcxbgdifebl_none_p_kernel(tc, x_words, x_scales, w1, sl, th, 
             return [pool.tile([P, width], F32, name=f"{name}{t}") for t in range(PACK)]
 
         xs_all = pool.tile([P, T], U8, name="xs_all")
-        nc.vector.memset(xs_all[:].bitcast(I32), 0)
+        nc.gpsimd.memset(xs_all[:].bitcast(I32), 0)
         offs_t = load_list("offs_t", offs)
         cand_t = load_list("cand_t", cand)
         for q in range(4):
@@ -58,22 +58,19 @@ def tile_picked_fkcdcxbgdifebl_none_p_kernel(tc, x_words, x_scales, w1, sl, th, 
         w1_raw = [load_weight_half(f"w1_raw{h}", w1, h) for h in range(2)]
         n4_t = load_list("n4_t", n4)
         n3_t = load_list("n3_t", n3)
-        n2_t = load_list("n2_t", n2)
         n1_t = load_list("n1_t", n1)
+        n2_t = load_list("n2_t", n2)
         w2_raw = [load_weight_half(f"w2_raw{h}", w2, h) for h in range(2)]
         n6_t = load_list("n6_t", n6)
         n5_t = load_list("n5_t", n5)
-        sl_t = load_rows("sl_t", sl)
-        th_t = load_rows("th_t", th)
-        gs_t = load_rows("gs_t", gs)
-        gn_t = load_rows("gn_t", gn)
-        y_win = planes("y_win", 2 * S)
-        for w in y_win:
-            nc.gpsimd.memset(w[:, S:], 0.0)
-        sl3_t = load_rows("sl3_t", sl3)
-        th3_t = load_rows("th3_t", th3)
-        sl2_t = load_rows("sl2_t", sl2)
-        th2_t = load_rows("th2_t", th2)
+        sl_t = load_rows("sl_t", sl, nc.gpsimd)
+        th_t = load_rows("th_t", th, nc.gpsimd)
+        gs_t = load_rows("gs_t", gs, nc.gpsimd)
+        gn_t = load_rows("gn_t", gn, nc.gpsimd)
+        sl3_t = load_rows("sl3_t", sl3, nc.sync)
+        th3_t = load_rows("th3_t", th3, nc.sync)
+        sl2_t = load_rows("sl2_t", sl2, nc.sync)
+        th2_t = load_rows("th2_t", th2, nc.sync)
 
         def sigmoid_bias(name, slope, threshold):
             prod = pool.tile([P, PACK], F32, name=name + "_prod")
@@ -83,10 +80,15 @@ def tile_picked_fkcdcxbgdifebl_none_p_kernel(tc, x_words, x_scales, w1, sl, th, 
             return bias
 
         bias_y = sigmoid_bias("bias_y", sl_t, th_t)
+        gn_neg = pool.tile([P, PACK], F32, name="gn_neg")
+        nc.gpsimd.tensor_scalar(gn_neg[:], gn_t[:], -1.0, 0.0, MULT, ADD)
         bias_b = sigmoid_bias("bias_b", sl3_t, th3_t)
         bias_a = sigmoid_bias("bias_a", sl2_t, th2_t)
 
         b_win = planes("b_win", 2 * S)
+        y_win = planes("y_win", 2 * S)
+        for w in y_win:
+            nc.vector.memset(w[:, S:], 0.0)
 
         xs = pool.tile([P, S], U8, name="xs", align_bytes=64)
         xw = pool.tile([P, S], U32, name="xw", align_bytes=64)
@@ -118,10 +120,10 @@ def tile_picked_fkcdcxbgdifebl_none_p_kernel(tc, x_words, x_scales, w1, sl, th, 
             nc.tensor.matmul_mx(bank[:], lhsT=lhs_codes.bitcast(FP8X4), lhsT_scale=lhs_scales,
                                 rhs=rhs_codes.bitcast(FP8X4), rhs_scale=rhs_scales, start=True, stop=True)
 
-        def interleave(mx, z):
+        def interleave(mx, z, c):
             nc.vector.tensor_copy(
-                mx[0][:].rearrange("p (c i t) -> p c t i", i=4, t=PACK),
-                z[:].rearrange("p t (c i) -> p c t i", i=4),
+                mx[0][:, PACK * c.start : PACK * c.stop].rearrange("p (c i t) -> p c t i", i=4, t=PACK),
+                z[:, :, c].rearrange("p t (c i) -> p c t i", i=4),
             )
 
         def weight_view(mx):
@@ -137,55 +139,87 @@ def tile_picked_fkcdcxbgdifebl_none_p_kernel(tc, x_words, x_scales, w1, sl, th, 
 
         sg, pa = planes("sg"), planes("pa")
         e = [w[:, S:] for w in b_win]
-        s2, yn = planes("s2"), planes("yn")
+        s2 = planes("s2")
         z2 = pool.tile([P, PACK, S], F32, name="z2")
-        z = pool.tile([P, PACK, S], F32, name="z")
+        z = z2
+        yn_early = pool.tile([P, 2, S], F32, name="yn_early")
+        yn = [yn_early[:, t, :] if t < 2 else z[:, t, :] for t in range(PACK)]
 
         def col(v, t):
             return v[:, t : t + 1]
 
+        y_copy = planes("y_copy")
         for t in range(PACK):
-            if t < 2:
-                nc.vector.tensor_copy(y_win[t][:, :S], y_ps[t][:])
-            else:
-                nc.scalar.copy(y_win[t][:, :S], y_ps[t][:])
+            (nc.vector.tensor_copy if t < 2 else nc.scalar.copy)(y_win[t][:, :S], y_ps[t][:])
+            nc.sync.dma_start(y_copy[t][:], y_win[t][:, :S])
             nc.scalar.activation(sg[t][:], y_win[t][:].indirect(n4_t[:]), SIGMOID, bias=col(bias_y, t), scale=col(sl_t, t))
-        for pair in ((0, 1), (2, 3)):
-            for t in pair:
-                nc.vector.tensor_copy(pa[t][:], y_win[t][:].indirect(n3_t[:]))
-            for t in pair:
-                nc.vector.tensor_tensor(e[t], y_ps[t][:], pa[t][:], SUB)
-            for t in pair:
-                nc.vector.scalar_tensor_tensor(e[t], e[t], col(gs_t, t), sg[t][:], MULT, MULT)
-            for t in pair:
-                nc.vector.scalar_tensor_tensor(z2[:, t, :], pa[t][:], col(gs_t, t), e[t], MULT, ADD)
+            nc.scalar.activation(pa[t][:], y_win[t][:].indirect(n3_t[:]), COPY)
         for t in range(PACK):
-            nc.scalar.activation(yn[t][:], y_win[t][:].indirect(n1_t[:]), COPY)
             nc.scalar.activation(s2[t][:], y_win[t][:].indirect(n2_t[:]), SIGMOID)
+
+        whole = slice(0, S)
+        halves = [slice(0, HALF), slice(HALF, S)]
+
+        def diff_pa(t):
+            nc.vector.tensor_tensor(e[t], y_ps[t][:], pa[t][:], SUB)
+
+        def gate_pa(t, c=whole):
+            nc.vector.scalar_tensor_tensor(e[t][:, c], e[t][:, c], col(gs_t, t), sg[t][:, c], MULT, MULT)
+
+        def blend(t, c=whole):
+            nc.vector.scalar_tensor_tensor(z2[:, t, c], pa[t][:, c], col(gs_t, t), e[t][:, c], MULT, ADD)
+
+        def diff_n1(t):
+            nc.vector.tensor_tensor(yn[t], y_win[t][:].indirect(n1_t[:]), y_copy[t][:], SUB)
+
+        def gate_n1(t, c=whole):
+            nc.vector.scalar_tensor_tensor(z[:, t, c], yn[t][:, c], col(gn_neg, t), s2[t][:, c], MULT, MULT)
+
+        def round_and_quantize(mx, planes4):
+            for c in halves:
+                interleave(mx, planes4, c)
+            for c in halves:
+                quantize(mx, c.start, c.stop)
 
         z2_mx = mx_tiles("z2")
         w2_mx = mx_tiles("w2")
-        interleave(z2_mx, z2)
-        deal_weight_half(nc.vector.tensor_copy, weight_view(w2_mx), w2_raw[0], 0)
-        quantize(z2_mx, 0, S)
+        z_mx = mx_tiles("z")
+        for h in range(2):
+            deal_weight_half(nc.vector.tensor_copy, weight_view(w2_mx), w2_raw[h], h)
+        diff_pa(0)
+        quantize(w2_mx, 0, S)
+        gate_pa(0)
+        diff_n1(0)
+        blend(0)
+        diff_pa(1)
+        diff_n1(1)
+        gate_pa(1)
+        diff_pa(2)
+        blend(1)
+        gate_pa(2)
+        diff_pa(3)
+        blend(2)
+        for c in halves:
+            gate_pa(3, c)
+        for c in halves:
+            blend(3, c)
+        round_and_quantize(z2_mx, z2)
         b_ps = [psum.tile([P, S], F32, name=f"b_ps{t}", tag=f"b{t}") for t in range(PACK)]
         for t in range(PACK):
             product(b_ps[t], cw[:, t, :], cs[:, t, :], z2_mx[1][:], z2_mx[2][:])
-        deal_weight_half(nc.vector.tensor_copy, weight_view(w2_mx), w2_raw[1], 1)
-        for t in range(PACK):
-            nc.vector.tensor_tensor(yn[t][:], y_ps[t][:], yn[t][:], SUB)
-        quantize(w2_mx, 0, S)
-        for t in range(PACK):
-            nc.vector.scalar_tensor_tensor(z[:, t, :], yn[t][:], col(gn_t, t), s2[t][:], MULT, MULT)
+        for t in range(2):
+            diff_n1(t + 2)
+            gate_n1(t)
+        gate_n1(2)
+        for c in halves:
+            gate_n1(3, c)
 
         sg3, sg2 = planes("sg3"), planes("sg2")
         for t in range(PACK):
             nc.scalar.activation(b_win[t][:, :S], b_ps[t][:], COPY, scale=0.0625)
             nc.scalar.activation(sg3[t][:], b_win[t][:].indirect(n6_t[:]), SIGMOID, bias=col(bias_b, t), scale=col(sl3_t, t))
 
-        z_mx = mx_tiles("z")
-        interleave(z_mx, z)
-        quantize(z_mx, 0, S)
+        round_and_quantize(z_mx, z)
         a_ps = [psum.tile([P, S], F32, name=f"a_ps{t}", tag=f"ya{t}") for t in range(PACK)]
         for t in range(PACK):
             product(a_ps[t], w2_mx[1][:, t * P : (t + 1) * P], w2_mx[2][:, t * P : (t + 1) * P], z_mx[1][:], z_mx[2][:])
@@ -194,14 +228,27 @@ def tile_picked_fkcdcxbgdifebl_none_p_kernel(tc, x_words, x_scales, w1, sl, th, 
         res = planes("res")
         out_rows = out.rearrange("(p t) n -> t p n", t=PACK)
         for t in range(PACK):
-            if t < 3:
-                nc.vector.tensor_copy(a_win[t][:, :S], a_ps[t][:])
-            else:
-                nc.scalar.copy(a_win[t][:, :S], a_ps[t][:])
-            nc.scalar.activation(sg2[t][:], a_win[t][:].indirect(n5_t[:]), SIGMOID, bias=col(bias_a, t), scale=col(sl2_t, t))
-        for t in range(PACK):
-            nc.vector.tensor_tensor(sg3[t][:], a_ps[t][:], sg3[t][:], MULT)
-            nc.vector.scalar_tensor_tensor(sg2[t][:], b_ps[t][:], 0.0625, sg2[t][:], MULT, MULT)
-            adder = nc.gpsimd if t < 3 else nc.vector
-            adder.tensor_tensor(res[t][:], sg2[t][:], sg3[t][:], ADD)
-            nc.sync.dma_start(out_rows[t], res[t][:])
+            nc.vector.tensor_copy(a_win[t][:, :S], a_ps[t][:])
+            for c in halves if t == 3 else [whole]:
+                nc.scalar.activation(sg2[t][:, c], a_win[t][:].indirect(n5_t[:, c.start // 16 : c.stop // 16]), SIGMOID,
+                                     bias=col(bias_a, t), scale=col(sl2_t, t))
+
+        def gate_b(t, c=whole):
+            nc.vector.scalar_tensor_tensor(sg2[t][:, c], b_ps[t][:, c], 0.0625, sg2[t][:, c], MULT, MULT)
+
+        def finish(adder, t, c=whole):
+            adder.tensor_tensor(res[t][:, c], sg2[t][:, c], sg3[t][:, c], ADD)
+            nc.sync.dma_start(out_rows[t][:, c], res[t][:, c])
+
+        for t in range(2):
+            nc.gpsimd.tensor_tensor(sg3[t][:], a_win[t][:, :S], sg3[t][:], MULT)
+        for t in range(2):
+            gate_b(t)
+            nc.vector.tensor_tensor(sg3[t + 2][:], a_ps[t + 2][:], sg3[t + 2][:], MULT)
+        gate_b(2)
+        for t in range(3):
+            finish(nc.gpsimd, t)
+        for c in halves:
+            gate_b(3, c)
+        for c in halves:
+            finish(nc.vector, 3, c)

@@ -56,21 +56,21 @@ def tile_picked_fkcdcxbgdifebl_none_p_kernel(tc, x_words, x_scales, w1, sl, th, 
         xw_all = pool.tile([P, T], I32, name="xw_all")
         nc.sync.dma_start(xw_all[:], x_words[0].rearrange("p n t -> p (n t)").bitcast(I32))
         w1_raw = [load_weight_half(f"w1_raw{h}", w1, h) for h in range(2)]
+        n2_t = load_list("n2_t", n2)
+        n1_t = load_list("n1_t", n1)
         n4_t = load_list("n4_t", n4)
         n3_t = load_list("n3_t", n3)
-        n1_t = load_list("n1_t", n1)
-        n2_t = load_list("n2_t", n2)
         w2_raw = [load_weight_half(f"w2_raw{h}", w2, h) for h in range(2)]
-        n6_t = load_list("n6_t", n6)
         n5_t = load_list("n5_t", n5)
+        n6_t = load_list("n6_t", n6)
+        gn_t = load_rows("gn_t", gn, nc.gpsimd)
         sl_t = load_rows("sl_t", sl, nc.gpsimd)
         th_t = load_rows("th_t", th, nc.gpsimd)
         gs_t = load_rows("gs_t", gs, nc.gpsimd)
-        gn_t = load_rows("gn_t", gn, nc.gpsimd)
-        sl3_t = load_rows("sl3_t", sl3, nc.sync)
-        th3_t = load_rows("th3_t", th3, nc.sync)
         sl2_t = load_rows("sl2_t", sl2, nc.sync)
         th2_t = load_rows("th2_t", th2, nc.sync)
+        sl3_t = load_rows("sl3_t", sl3, nc.sync)
+        th3_t = load_rows("th3_t", th3, nc.sync)
 
         def sigmoid_bias(name, slope, threshold):
             prod = pool.tile([P, PACK], F32, name=name + "_prod")
@@ -85,7 +85,7 @@ def tile_picked_fkcdcxbgdifebl_none_p_kernel(tc, x_words, x_scales, w1, sl, th, 
         bias_b = sigmoid_bias("bias_b", sl3_t, th3_t)
         bias_a = sigmoid_bias("bias_a", sl2_t, th2_t)
 
-        b_win = planes("b_win", 2 * S)
+        a_win = planes("a_win", 2 * S)
         y_win = planes("y_win", 2 * S)
         for w in y_win:
             nc.vector.memset(w[:, S:], 0.0)
@@ -106,9 +106,9 @@ def tile_picked_fkcdcxbgdifebl_none_p_kernel(tc, x_words, x_scales, w1, sl, th, 
                 raw[:].rearrange("p j (m t) -> p m j t", t=PACK),
             )
 
-        def mx_tiles(name):
-            grouped = pool.tile([P, PACK * S], BF16, name=name + "_bf", align_bytes=64)
-            codes = pool.tile([P, S], U32, name=name + "_codes", align_bytes=64)
+        def mx_tiles(name, grouped_tag=None, codes_tag=None):
+            grouped = pool.tile([P, PACK * S], BF16, name=name + "_bf", tag=grouped_tag or name + "_bf", align_bytes=64)
+            codes = pool.tile([P, S], U32, name=name + "_codes", tag=codes_tag or name + "_codes", align_bytes=64)
             scales = pool.tile([P, S], U8, name=name + "_scales", align_bytes=64)
             return grouped, codes, scales
 
@@ -129,33 +129,44 @@ def tile_picked_fkcdcxbgdifebl_none_p_kernel(tc, x_words, x_scales, w1, sl, th, 
         def weight_view(mx):
             return mx[0][:].rearrange("p (t m j) -> p t m j", t=PACK, j=PACK)
 
-        w1_mx = mx_tiles("w1")
+        w1_mx = mx_tiles("w1", codes_tag="w1_codes_then_w2_bf")
         deal_weight_half(nc.scalar.copy, weight_view(w1_mx), w1_raw[0], 0)
         deal_weight_half(nc.vector.tensor_copy, weight_view(w1_mx), w1_raw[1], 1)
-        y_ps = [psum.tile([P, S], F32, name=f"y_ps{t}", tag=f"ya{t}") for t in range(PACK)]
+        y_ps = [psum.tile([P, S], F32, name=f"y_ps{t}", tag=f"yb{t}") for t in range(PACK)]
         for t in range(PACK):
             quantize(w1_mx, t * P, (t + 1) * P)
             product(y_ps[t], w1_mx[1][:, t * P : (t + 1) * P], w1_mx[2][:, t * P : (t + 1) * P], xw[:], xs[:])
 
-        sg, pa = planes("sg"), planes("pa")
-        e = [w[:, S:] for w in b_win]
-        s2 = planes("s2")
+        sg, pa, s2 = planes("sg"), planes("pa"), planes("s2")
+        yn = [w[:, S:] for w in a_win]
+        z = pool.tile([P, PACK, S], F32, name="z")
         z2 = pool.tile([P, PACK, S], F32, name="z2")
-        z = z2
-        yn_early = pool.tile([P, 2, S], F32, name="yn_early")
-        yn = [yn_early[:, t, :] if t < 2 else z[:, t, :] for t in range(PACK)]
+        e = [z[:, t, :] for t in range(PACK)]
 
         def col(v, t):
             return v[:, t : t + 1]
 
         y_copy = planes("y_copy")
-        for t in range(PACK):
-            (nc.vector.tensor_copy if t < 2 else nc.scalar.copy)(y_win[t][:, :S], y_ps[t][:])
+
+        def keep_y(copy, t):
+            copy(y_win[t][:, :S], y_ps[t][:])
             nc.sync.dma_start(y_copy[t][:], y_win[t][:, :S])
+
+        def fetch_sg(t):
             nc.scalar.activation(sg[t][:], y_win[t][:].indirect(n4_t[:]), SIGMOID, bias=col(bias_y, t), scale=col(sl_t, t))
+
+        def fetch_pa(t):
             nc.scalar.activation(pa[t][:], y_win[t][:].indirect(n3_t[:]), COPY)
-        for t in range(PACK):
+
+        def fetch_s2(t):
             nc.scalar.activation(s2[t][:], y_win[t][:].indirect(n2_t[:]), SIGMOID)
+
+        for t in range(PACK):
+            keep_y(nc.vector.tensor_copy, t)
+            fetch_s2(t)
+        for t in range(PACK):
+            fetch_pa(t)
+            fetch_sg(t)
 
         whole = slice(0, S)
         halves = [slice(0, HALF), slice(HALF, S)]
@@ -182,73 +193,74 @@ def tile_picked_fkcdcxbgdifebl_none_p_kernel(tc, x_words, x_scales, w1, sl, th, 
                 quantize(mx, c.start, c.stop)
 
         z2_mx = mx_tiles("z2")
-        w2_mx = mx_tiles("w2")
+        w2_mx = mx_tiles("w2", grouped_tag="w1_codes_then_w2_bf")
         z_mx = mx_tiles("z")
         for h in range(2):
             deal_weight_half(nc.vector.tensor_copy, weight_view(w2_mx), w2_raw[h], h)
-        diff_pa(0)
         quantize(w2_mx, 0, S)
-        gate_pa(0)
         diff_n1(0)
-        blend(0)
+        for t in range(1, PACK):
+            diff_n1(t)
+            gate_n1(t - 1)
+        for c in halves:
+            gate_n1(3, c)
+        round_and_quantize(z_mx, z)
+        a_ps = [psum.tile([P, S], F32, name=f"a_ps{t}", tag=f"a{t}") for t in range(PACK)]
+        for t in range(PACK):
+            product(a_ps[t], w2_mx[1][:, t * P : (t + 1) * P], w2_mx[2][:, t * P : (t + 1) * P], z_mx[1][:], z_mx[2][:])
+
+        diff_pa(0)
         diff_pa(1)
-        diff_n1(1)
-        gate_pa(1)
-        diff_pa(2)
-        blend(1)
-        gate_pa(2)
-        diff_pa(3)
-        blend(2)
+        for t in range(PACK - 1):
+            gate_pa(t)
+            if t + 2 < PACK:
+                diff_pa(t + 2)
+            blend(t)
         for c in halves:
             gate_pa(3, c)
         for c in halves:
             blend(3, c)
+
+        sg2, sg3 = planes("sg2"), planes("sg3")
+
+        def fetch_sg2(t):
+            nc.scalar.activation(sg2[t][:], a_win[t][:].indirect(n5_t[:]), SIGMOID, bias=col(bias_a, t), scale=col(sl2_t, t))
+
+        nc.scalar.copy(a_win[0][:, :S], a_ps[0][:])
+        for t in range(PACK):
+            if t + 1 < PACK:
+                nc.scalar.copy(a_win[t + 1][:, :S], a_ps[t + 1][:])
+            fetch_sg2(t)
+
         round_and_quantize(z2_mx, z2)
-        b_ps = [psum.tile([P, S], F32, name=f"b_ps{t}", tag=f"b{t}") for t in range(PACK)]
+        b_ps = [psum.tile([P, S], F32, name=f"b_ps{t}", tag=f"yb{t}") for t in range(PACK)]
         for t in range(PACK):
             product(b_ps[t], cw[:, t, :], cs[:, t, :], z2_mx[1][:], z2_mx[2][:])
-        for t in range(2):
-            diff_n1(t + 2)
-            gate_n1(t)
-        gate_n1(2)
-        for c in halves:
-            gate_n1(3, c)
 
-        sg3, sg2 = planes("sg3"), planes("sg2")
-        for t in range(PACK):
-            nc.scalar.activation(b_win[t][:, :S], b_ps[t][:], COPY, scale=0.0625)
-            nc.scalar.activation(sg3[t][:], b_win[t][:].indirect(n6_t[:]), SIGMOID, bias=col(bias_b, t), scale=col(sl3_t, t))
-
-        round_and_quantize(z_mx, z)
-        a_ps = [psum.tile([P, S], F32, name=f"a_ps{t}", tag=f"ya{t}") for t in range(PACK)]
-        for t in range(PACK):
-            product(a_ps[t], w2_mx[1][:, t * P : (t + 1) * P], w2_mx[2][:, t * P : (t + 1) * P], z_mx[1][:], z_mx[2][:])
-
-        a_win = y_win
+        b_win = y_win
         res = planes("res")
         out_rows = out.rearrange("(p t) n -> t p n", t=PACK)
         for t in range(PACK):
-            nc.vector.tensor_copy(a_win[t][:, :S], a_ps[t][:])
+            nc.vector.tensor_scalar_mul(b_win[t][:, :S], b_ps[t][:], 0.0625)
             for c in halves if t == 3 else [whole]:
-                nc.scalar.activation(sg2[t][:, c], a_win[t][:].indirect(n5_t[:, c.start // 16 : c.stop // 16]), SIGMOID,
-                                     bias=col(bias_a, t), scale=col(sl2_t, t))
+                nc.scalar.activation(sg3[t][:, c], b_win[t][:].indirect(n6_t[:, c.start // 16 : c.stop // 16]), SIGMOID,
+                                     bias=col(bias_b, t), scale=col(sl3_t, t))
 
-        def gate_b(t, c=whole):
-            nc.vector.scalar_tensor_tensor(sg2[t][:, c], b_ps[t][:, c], 0.0625, sg2[t][:, c], MULT, MULT)
+        def gate_a(t, c=whole):
+            nc.vector.tensor_tensor(sg3[t][:, c], a_ps[t][:, c], sg3[t][:, c], MULT)
 
         def finish(adder, t, c=whole):
             adder.tensor_tensor(res[t][:, c], sg2[t][:, c], sg3[t][:, c], ADD)
             nc.sync.dma_start(out_rows[t][:, c], res[t][:, c])
 
         for t in range(2):
-            nc.gpsimd.tensor_tensor(sg3[t][:], a_win[t][:, :S], sg3[t][:], MULT)
+            nc.gpsimd.tensor_tensor(sg2[t][:], b_win[t][:, :S], sg2[t][:], MULT)
         for t in range(2):
-            gate_b(t)
-            nc.vector.tensor_tensor(sg3[t + 2][:], a_ps[t + 2][:], sg3[t + 2][:], MULT)
-        gate_b(2)
+            gate_a(t)
+            nc.vector.scalar_tensor_tensor(sg2[t + 2][:], b_ps[t + 2][:], 0.0625, sg2[t + 2][:], MULT, MULT)
+        gate_a(2)
         for t in range(3):
             finish(nc.gpsimd, t)
         for c in halves:
-            gate_b(3, c)
-        for c in halves:
+            gate_a(3, c)
             finish(nc.vector, 3, c)

@@ -93,22 +93,20 @@ def tile_picked_fkcdcxbgdifebl_none_p_kernel(tc, x_words, x_scales, w1, sl, th, 
         xs = pool.tile([P, S], U8, name="xs", align_bytes=64)
         xw = pool.tile([P, S], U32, name="xw", align_bytes=64)
         cs = pool.tile([P, PACK, P], U8, name="cs", align_bytes=64)
-        cw = pool.tile([P, PACK, P], U32, name="cw", align_bytes=64)
         nc.vector.tensor_copy(xs[:], xs_all[:].indirect(offs_t[:]))
         nc.vector.tensor_copy(cs[:].rearrange("p t m -> p m t"), xs_all[:].indirect(cand_t[:]))
         nc.vector.tensor_copy(xw[:], xw_all[:].bitcast(U32).indirect(offs_t[:]))
-        nc.vector.tensor_copy(cw[:].rearrange("p t m -> p m t"), xw_all[:].bitcast(U32).indirect(cand_t[:]))
 
-        def deal_weight_half(copy, grouped, raw, h):
-            m = HALF // PACK
+        def deal_weight(copy, grouped, raw, h, lo=0, hi=HALF // PACK):
+            m0 = h * HALF // PACK
             copy(
-                grouped[:, :, h * m : (h + 1) * m, :].rearrange("p t m j -> p m j t"),
-                raw[:].rearrange("p j (m t) -> p m j t", t=PACK),
+                grouped[:].rearrange("p (t m j) -> p m j t", t=PACK, j=PACK)[:, m0 + lo : m0 + hi],
+                raw[:].rearrange("p j (m t) -> p m j t", t=PACK)[:, lo:hi],
             )
 
-        def mx_tiles(name, grouped_tag=None, codes_tag=None):
+        def mx_tiles(name, grouped_tag=None):
             grouped = pool.tile([P, PACK * S], BF16, name=name + "_bf", tag=grouped_tag or name + "_bf", align_bytes=64)
-            codes = pool.tile([P, S], U32, name=name + "_codes", tag=codes_tag or name + "_codes", align_bytes=64)
+            codes = pool.tile([P, S], U32, name=name + "_codes", align_bytes=64)
             scales = pool.tile([P, S], U8, name=name + "_scales", align_bytes=64)
             return grouped, codes, scales
 
@@ -117,7 +115,7 @@ def tile_picked_fkcdcxbgdifebl_none_p_kernel(tc, x_words, x_scales, w1, sl, th, 
             nc.vector.quantize_mx(codes[:, lo:hi].bitcast(FP8X4), scales[:, lo:hi], grouped[:, PACK * lo : PACK * hi])
 
         def product(bank, lhs_codes, lhs_scales, rhs_codes, rhs_scales):
-            nc.tensor.matmul_mx(bank[:], lhsT=lhs_codes.bitcast(FP8X4), lhsT_scale=lhs_scales,
+            nc.tensor.matmul_mx(bank, lhsT=lhs_codes.bitcast(FP8X4), lhsT_scale=lhs_scales,
                                 rhs=rhs_codes.bitcast(FP8X4), rhs_scale=rhs_scales, start=True, stop=True)
 
         def interleave(mx, z, c):
@@ -126,16 +124,16 @@ def tile_picked_fkcdcxbgdifebl_none_p_kernel(tc, x_words, x_scales, w1, sl, th, 
                 z[:, :, c].rearrange("p t (c i) -> p c t i", i=4),
             )
 
-        def weight_view(mx):
-            return mx[0][:].rearrange("p (t m j) -> p t m j", t=PACK, j=PACK)
-
-        w1_mx = mx_tiles("w1", codes_tag="w1_codes_then_w2_bf")
-        deal_weight_half(nc.scalar.copy, weight_view(w1_mx), w1_raw[0], 0)
-        deal_weight_half(nc.vector.tensor_copy, weight_view(w1_mx), w1_raw[1], 1)
+        w1_bf = pool.tile([P, PACK * S], BF16, name="w1_bf", align_bytes=64)
+        deal_weight(nc.scalar.copy, w1_bf, w1_raw[0], 0, 0, 32)
+        deal_weight(nc.vector.tensor_copy, w1_bf, w1_raw[0], 0, 32, 64)
+        deal_weight(nc.vector.tensor_copy, w1_bf, w1_raw[1], 1)
         y_ps = [psum.tile([P, S], F32, name=f"y_ps{t}", tag=f"yb{t}") for t in range(PACK)]
         for t in range(PACK):
-            quantize(w1_mx, t * P, (t + 1) * P)
-            product(y_ps[t], w1_mx[1][:, t * P : (t + 1) * P], w1_mx[2][:, t * P : (t + 1) * P], xw[:], xs[:])
+            codes = pool.tile([P, P], U32, name=f"w1_codes{t}", align_bytes=64)
+            scales = pool.tile([P, P], U8, name=f"w1_scales{t}", align_bytes=64)
+            nc.vector.quantize_mx(codes[:].bitcast(FP8X4), scales[:], w1_bf[:, t * S : (t + 1) * S])
+            product(y_ps[t][:], codes[:], scales[:], xw[:], xs[:])
 
         sg, pa, s2 = planes("sg"), planes("pa"), planes("s2")
         yn = [w[:, S:] for w in a_win]
@@ -161,8 +159,12 @@ def tile_picked_fkcdcxbgdifebl_none_p_kernel(tc, x_words, x_scales, w1, sl, th, 
         def fetch_s2(t):
             nc.scalar.activation(s2[t][:], y_win[t][:].indirect(n2_t[:]), SIGMOID)
 
-        for t in range(PACK):
+        for t in range(2):
             keep_y(nc.vector.tensor_copy, t)
+        fetch_s2(0)
+        for t in range(1, PACK):
+            if t + 1 < PACK:
+                keep_y(nc.scalar.copy, t + 1)
             fetch_s2(t)
         for t in range(PACK):
             fetch_pa(t)
@@ -193,10 +195,12 @@ def tile_picked_fkcdcxbgdifebl_none_p_kernel(tc, x_words, x_scales, w1, sl, th, 
                 quantize(mx, c.start, c.stop)
 
         z2_mx = mx_tiles("z2")
-        w2_mx = mx_tiles("w2", grouped_tag="w1_codes_then_w2_bf")
+        w2_mx = mx_tiles("w2", grouped_tag="w1_codes0")
+        cw = pool.tile([P, PACK, P], U32, name="cw", tag="w1_scales0", align_bytes=64)
+        nc.vector.tensor_copy(cw[:].rearrange("p t m -> p m t"), xw_all[:].bitcast(U32).indirect(cand_t[:]))
         z_mx = mx_tiles("z")
         for h in range(2):
-            deal_weight_half(nc.vector.tensor_copy, weight_view(w2_mx), w2_raw[h], h)
+            deal_weight(nc.vector.tensor_copy, w2_mx[0], w2_raw[h], h)
         quantize(w2_mx, 0, S)
         diff_n1(0)
         for t in range(1, PACK):
@@ -207,7 +211,7 @@ def tile_picked_fkcdcxbgdifebl_none_p_kernel(tc, x_words, x_scales, w1, sl, th, 
         round_and_quantize(z_mx, z)
         a_ps = [psum.tile([P, S], F32, name=f"a_ps{t}", tag=f"a{t}") for t in range(PACK)]
         for t in range(PACK):
-            product(a_ps[t], w2_mx[1][:, t * P : (t + 1) * P], w2_mx[2][:, t * P : (t + 1) * P], z_mx[1][:], z_mx[2][:])
+            product(a_ps[t][:], w2_mx[1][:, t * P : (t + 1) * P], w2_mx[2][:, t * P : (t + 1) * P], z_mx[1][:], z_mx[2][:])
 
         diff_pa(0)
         diff_pa(1)
@@ -235,7 +239,8 @@ def tile_picked_fkcdcxbgdifebl_none_p_kernel(tc, x_words, x_scales, w1, sl, th, 
         round_and_quantize(z2_mx, z2)
         b_ps = [psum.tile([P, S], F32, name=f"b_ps{t}", tag=f"yb{t}") for t in range(PACK)]
         for t in range(PACK):
-            product(b_ps[t], cw[:, t, :], cs[:, t, :], z2_mx[1][:], z2_mx[2][:])
+            for c in halves if t == 0 else [whole]:
+                product(b_ps[t][:, c], cw[:, t, :], cs[:, t, :], z2_mx[1][:, c], z2_mx[2][:, c])
 
         b_win = y_win
         res = planes("res")
@@ -263,4 +268,5 @@ def tile_picked_fkcdcxbgdifebl_none_p_kernel(tc, x_words, x_scales, w1, sl, th, 
             finish(nc.gpsimd, t)
         for c in halves:
             gate_a(3, c)
+        for c in halves:
             finish(nc.vector, 3, c)

@@ -82,8 +82,6 @@ def tile_picked_fkcdcxbgdifebl_none_p_kernel(tc, x_words, x_scales, w1, sl, th, 
         bias_y = sigmoid_bias("bias_y", sl_t, th_t)
         gn_neg = pool.tile([P, PACK], F32, name="gn_neg")
         nc.gpsimd.tensor_scalar(gn_neg[:], gn_t[:], -1.0, 0.0, MULT, ADD)
-        bias_b = sigmoid_bias("bias_b", sl3_t, th3_t)
-        bias_a = sigmoid_bias("bias_a", sl2_t, th2_t)
 
         a_win = planes("a_win", 2 * S)
         y_win = planes("y_win", 2 * S)
@@ -103,6 +101,10 @@ def tile_picked_fkcdcxbgdifebl_none_p_kernel(tc, x_words, x_scales, w1, sl, th, 
                 grouped[:].rearrange("p (t m j) -> p m j t", t=PACK, j=PACK)[:, m0 + lo : m0 + hi],
                 raw[:].rearrange("p j (m t) -> p m j t", t=PACK)[:, lo:hi],
             )
+
+        def gpsimd_round(dst, src):
+            order = "p m j t -> p m t j"
+            nc.gpsimd.tensor_scalar(dst.rearrange(order), src.rearrange(order), 1.0, 0.0, MULT, ADD)
 
         def mx_tiles(name, grouped_tag=None):
             grouped = pool.tile([P, PACK * S], BF16, name=name + "_bf", tag=grouped_tag or name + "_bf", align_bytes=64)
@@ -159,12 +161,8 @@ def tile_picked_fkcdcxbgdifebl_none_p_kernel(tc, x_words, x_scales, w1, sl, th, 
         def fetch_s2(t):
             nc.scalar.activation(s2[t][:], y_win[t][:].indirect(n2_t[:]), SIGMOID)
 
-        for t in range(2):
+        for t in range(PACK):
             keep_y(nc.vector.tensor_copy, t)
-        fetch_s2(0)
-        for t in range(1, PACK):
-            if t + 1 < PACK:
-                keep_y(nc.scalar.copy, t + 1)
             fetch_s2(t)
         for t in range(PACK):
             fetch_pa(t)
@@ -196,13 +194,15 @@ def tile_picked_fkcdcxbgdifebl_none_p_kernel(tc, x_words, x_scales, w1, sl, th, 
 
         z2_mx = mx_tiles("z2")
         w2_mx = mx_tiles("w2", grouped_tag="w1_codes0")
-        cw = pool.tile([P, PACK, P], U32, name="cw", tag="w1_scales0", align_bytes=64)
+        cw = pool.tile([P, PACK, P], U32, name="cw", tag="w1_scales3", align_bytes=64)
         nc.vector.tensor_copy(cw[:].rearrange("p t m -> p m t"), xw_all[:].bitcast(U32).indirect(cand_t[:]))
         z_mx = mx_tiles("z")
         for h in range(2):
-            deal_weight(nc.vector.tensor_copy, w2_mx[0], w2_raw[h], h)
-        quantize(w2_mx, 0, S)
+            deal_weight(gpsimd_round, w2_mx[0], w2_raw[h], h)
+        bias_a = sigmoid_bias("bias_a", sl2_t, th2_t)
+        bias_b = sigmoid_bias("bias_b", sl3_t, th3_t)
         diff_n1(0)
+        quantize(w2_mx, 0, S)
         for t in range(1, PACK):
             diff_n1(t)
             gate_n1(t - 1)

from contextlib import ExitStack

import concourse.mybir as mybir

F32 = mybir.dt.float32
BF16 = mybir.dt.bfloat16
I32 = mybir.dt.int32
U32 = mybir.dt.uint32
U16 = mybir.dt.uint16
U8 = mybir.dt.uint8
FP8X4 = mybir.dt.float8_e4m3fn_x4
MULT = mybir.AluOpType.mult
ADD = mybir.AluOpType.add
SUB = mybir.AluOpType.subtract
SIGMOID = mybir.ActivationFunctionType.Sigmoid
COPY = mybir.ActivationFunctionType.Copy

P = 128
PACK = 4
T = 2048
S = 512
HALF = S // 2
FLOPS = 3 * 2 * 512 * 512 * 512


def tile_picked_fkcdcxbgdifebl_none_p_kernel(tc, x_words, x_scales, w1, sl, th, gn, w2, gs, sl2, th2, sl3, th3, offs, n1, n2, n3, n4, cand, n5, n6, out):
    nc = tc.nc
    with ExitStack() as ctx:
        pool = ctx.enter_context(tc.tile_pool(name="sbuf", bufs=1))
        psum = ctx.enter_context(tc.psum_pool(name="psum", bufs=1))

        def load_list(name, src):
            t = pool.tile([P, S // 16], U16, name=name)
            nc.sync.dma_start(t[:], src)
            return t

        def load_rows(name, src, queue):
            t = pool.tile([P, PACK], F32, name=name)
            queue.dma_start(t[:], src.rearrange("(p t) o -> p (t o)", t=PACK))
            return t

        def load_weight_half(name, w, h):
            t = pool.tile([P, PACK, HALF], F32, name=name)
            nc.sync.dma_start(t[:], w.rearrange("(p j) c -> p j c", j=PACK)[:, :, h * HALF : (h + 1) * HALF])
            return t

        def planes(name, width=S):
            return [pool.tile([P, width], F32, name=f"{name}{t}") for t in range(PACK)]

        xs_all = pool.tile([P, T], U8, name="xs_all")
        nc.gpsimd.memset(xs_all[:].bitcast(I32), 0)
        offs_t = load_list("offs_t", offs)
        cand_t = load_list("cand_t", cand)
        for q in range(4):
            nc.sync.dma_start(xs_all[32 * q : 32 * q + 4, :].bitcast(I32), x_scales[0, 4 * q : 4 * q + 4, :].bitcast(I32))
        xw_all = pool.tile([P, T], I32, name="xw_all")
        nc.sync.dma_start(xw_all[:], x_words[0].rearrange("p n t -> p (n t)").bitcast(I32))
        w1_raw = [load_weight_half(f"w1_raw{h}", w1, h) for h in range(2)]
        n2_t = load_list("n2_t", n2)
        n1_t = load_list("n1_t", n1)
        n4_t = load_list("n4_t", n4)
        n3_t = load_list("n3_t", n3)
        w2_raw = [load_weight_half(f"w2_raw{h}", w2, h) for h in range(2)]
        n5_t = load_list("n5_t", n5)
        n6_t = load_list("n6_t", n6)
        gn_t = load_rows("gn_t", gn, nc.gpsimd)
        sl_t = load_rows("sl_t", sl, nc.gpsimd)
        th_t = load_rows("th_t", th, nc.gpsimd)
        gs_t = load_rows("gs_t", gs, nc.gpsimd)
        sl2_t = load_rows("sl2_t", sl2, nc.sync)
        th2_t = load_rows("th2_t", th2, nc.sync)
        sl3_t = load_rows("sl3_t", sl3, nc.sync)
        th3_t = load_rows("th3_t", th3, nc.sync)

        def sigmoid_bias(name, slope, threshold):
            prod = pool.tile([P, PACK], F32, name=name + "_prod")
            bias = pool.tile([P, PACK], F32, name=name)
            nc.gpsimd.tensor_tensor(prod[:], slope[:], threshold[:], MULT)
            nc.gpsimd.tensor_scalar(bias[:], prod[:], -1.0, 0.0, MULT, ADD)
            return bias

        bias_y = sigmoid_bias("bias_y", sl_t, th_t)
        gn_neg = pool.tile([P, PACK], F32, name="gn_neg")
        nc.gpsimd.tensor_scalar(gn_neg[:], gn_t[:], -1.0, 0.0, MULT, ADD)

        a_win = planes("a_win", 2 * S)
        y_win = planes("y_win", 2 * S)
        for w in y_win:
            nc.vector.memset(w[:, S:], 0.0)

        xs = pool.tile([P, S], U8, name="xs", align_bytes=64)
        xw = pool.tile([P, S], U32, name="xw", align_bytes=64)
        cs = pool.tile([P, PACK, P], U8, name="cs", align_bytes=64)
        nc.vector.tensor_copy(xs[:], xs_all[:].indirect(offs_t[:]))
        nc.vector.tensor_copy(cs[:].rearrange("p t m -> p m t"), xs_all[:].indirect(cand_t[:]))
        nc.vector.tensor_copy(xw[:], xw_all[:].bitcast(U32).indirect(offs_t[:]))

        def deal_weight(copy, grouped, raw, h, lo=0, hi=HALF // PACK):
            m0 = h * HALF // PACK
            copy(
                grouped[:].rearrange("p (t m j) -> p m j t", t=PACK, j=PACK)[:, m0 + lo : m0 + hi],
                raw[:].rearrange("p j (m t) -> p m j t", t=PACK)[:, lo:hi],
            )

        def gpsimd_round(dst, src):
            order = "p m j t -> p m t j"
            nc.gpsimd.tensor_scalar(dst.rearrange(order), src.rearrange(order), 1.0, 0.0, MULT, ADD)

        def mx_tiles(name, grouped_tag=None):
            grouped = pool.tile([P, PACK * S], BF16, name=name + "_bf", tag=grouped_tag or name + "_bf", align_bytes=64)
            codes = pool.tile([P, S], U32, name=name + "_codes", align_bytes=64)
            scales = pool.tile([P, S], U8, name=name + "_scales", align_bytes=64)
            return grouped, codes, scales

        def quantize(mx, lo, hi):
            grouped, codes, scales = mx
            nc.vector.quantize_mx(codes[:, lo:hi].bitcast(FP8X4), scales[:, lo:hi], grouped[:, PACK * lo : PACK * hi])

        def product(bank, lhs_codes, lhs_scales, rhs_codes, rhs_scales):
            nc.tensor.matmul_mx(bank, lhsT=lhs_codes.bitcast(FP8X4), lhsT_scale=lhs_scales,
                                rhs=rhs_codes.bitcast(FP8X4), rhs_scale=rhs_scales, start=True, stop=True)

        def interleave(mx, z, c):
            nc.vector.tensor_copy(
                mx[0][:, PACK * c.start : PACK * c.stop].rearrange("p (c i t) -> p c t i", i=4, t=PACK),
                z[:, :, c].rearrange("p t (c i) -> p c t i", i=4),
            )

        w1_bf = pool.tile([P, PACK * S], BF16, name="w1_bf", align_bytes=64)
        deal_weight(nc.scalar.copy, w1_bf, w1_raw[0], 0, 0, 32)
        deal_weight(nc.vector.tensor_copy, w1_bf, w1_raw[0], 0, 32, 64)
        deal_weight(nc.vector.tensor_copy, w1_bf, w1_raw[1], 1)
        y_ps = [psum.tile([P, S], F32, name=f"y_ps{t}", tag=f"yb{t}") for t in range(PACK)]
        for t in range(PACK):
            codes = pool.tile([P, P], U32, name=f"w1_codes{t}", align_bytes=64)
            scales = pool.tile([P, P], U8, name=f"w1_scales{t}", align_bytes=64)
            nc.vector.quantize_mx(codes[:].bitcast(FP8X4), scales[:], w1_bf[:, t * S : (t + 1) * S])
            product(y_ps[t][:], codes[:], scales[:], xw[:], xs[:])

        sg, pa, s2 = planes("sg"), planes("pa"), planes("s2")
        yn = [w[:, S:] for w in a_win]
        z = pool.tile([P, PACK, S], F32, name="z")
        z2 = pool.tile([P, PACK, S], F32, name="z2")
        e = [z[:, t, :] for t in range(PACK)]

        def col(v, t):
            return v[:, t : t + 1]

        y_copy = planes("y_copy")

        def keep_y(copy, t):
            copy(y_win[t][:, :S], y_ps[t][:])
            nc.sync.dma_start(y_copy[t][:], y_win[t][:, :S])

        def fetch_sg(t):
            nc.scalar.activation(sg[t][:], y_win[t][:].indirect(n4_t[:]), SIGMOID, bias=col(bias_y, t), scale=col(sl_t, t))

        def fetch_pa(t):
            nc.scalar.activation(pa[t][:], y_win[t][:].indirect(n3_t[:]), COPY)

        def fetch_s2(t):
            nc.scalar.activation(s2[t][:], y_win[t][:].indirect(n2_t[:]), SIGMOID)

        for t in range(PACK):
            keep_y(nc.vector.tensor_copy, t)
            fetch_s2(t)
        for t in range(PACK):
            fetch_pa(t)
            fetch_sg(t)

        whole = slice(0, S)
        halves = [slice(0, HALF), slice(HALF, S)]

        def diff_pa(t):
            nc.vector.tensor_tensor(e[t], y_ps[t][:], pa[t][:], SUB)

        def gate_pa(t, c=whole):
            nc.vector.scalar_tensor_tensor(e[t][:, c], e[t][:, c], col(gs_t, t), sg[t][:, c], MULT, MULT)

        def blend(t, c=whole):
            nc.vector.scalar_tensor_tensor(z2[:, t, c], pa[t][:, c], col(gs_t, t), e[t][:, c], MULT, ADD)

        def diff_n1(t):
            nc.vector.tensor_tensor(yn[t], y_win[t][:].indirect(n1_t[:]), y_copy[t][:], SUB)

        def gate_n1(t, c=whole):
            nc.vector.scalar_tensor_tensor(z[:, t, c], yn[t][:, c], col(gn_neg, t), s2[t][:, c], MULT, MULT)

        def round_and_quantize(mx, planes4):
            for c in halves:
                interleave(mx, planes4, c)
            for c in halves:
                quantize(mx, c.start, c.stop)

        z2_mx = mx_tiles("z2")
        w2_mx = mx_tiles("w2", grouped_tag="w1_codes0")
        cw = pool.tile([P, PACK, P], U32, name="cw", tag="w1_scales3", align_bytes=64)
        nc.vector.tensor_copy(cw[:].rearrange("p t m -> p m t"), xw_all[:].bitcast(U32).indirect(cand_t[:]))
        z_mx = mx_tiles("z")
        for h in range(2):
            deal_weight(gpsimd_round, w2_mx[0], w2_raw[h], h)
        bias_a = sigmoid_bias("bias_a", sl2_t, th2_t)
        bias_b = sigmoid_bias("bias_b", sl3_t, th3_t)
        diff_n1(0)
        quantize(w2_mx, 0, S)
        for t in range(1, PACK):
            diff_n1(t)
            gate_n1(t - 1)
        for c in halves:
            gate_n1(3, c)
        round_and_quantize(z_mx, z)
        a_ps = [psum.tile([P, S], F32, name=f"a_ps{t}", tag=f"a{t}") for t in range(PACK)]
        for t in range(PACK):
            product(a_ps[t][:], w2_mx[1][:, t * P : (t + 1) * P], w2_mx[2][:, t * P : (t + 1) * P], z_mx[1][:], z_mx[2][:])

        diff_pa(0)
        diff_pa(1)
        for t in range(PACK - 1):
            gate_pa(t)
            if t + 2 < PACK:
                diff_pa(t + 2)
            blend(t)
        for c in halves:
            gate_pa(3, c)
        for c in halves:
            blend(3, c)

        sg2, sg3 = planes("sg2"), planes("sg3")

        def fetch_sg2(t):
            nc.scalar.activation(sg2[t][:], a_win[t][:].indirect(n5_t[:]), SIGMOID, bias=col(bias_a, t), scale=col(sl2_t, t))

        nc.scalar.copy(a_win[0][:, :S], a_ps[0][:])
        for t in range(PACK):
            if t + 1 < PACK:
                nc.scalar.copy(a_win[t + 1][:, :S], a_ps[t + 1][:])
            fetch_sg2(t)

        round_and_quantize(z2_mx, z2)
        b_ps = [psum.tile([P, S], F32, name=f"b_ps{t}", tag=f"yb{t}") for t in range(PACK)]
        for t in range(PACK):
            for c in halves if t == 0 else [whole]:
                product(b_ps[t][:, c], cw[:, t, :], cs[:, t, :], z2_mx[1][:, c], z2_mx[2][:, c])

        b_win = y_win
        res = planes("res")
        out_rows = out.rearrange("(p t) n -> t p n", t=PACK)
        for t in range(PACK):
            nc.vector.tensor_scalar_mul(b_win[t][:, :S], b_ps[t][:], 0.0625)
            for c in halves if t == 3 else [whole]:
                nc.scalar.activation(sg3[t][:, c], b_win[t][:].indirect(n6_t[:, c.start // 16 : c.stop // 16]), SIGMOID,
                                     bias=col(bias_b, t), scale=col(sl3_t, t))

        def gate_a(t, c=whole):
            nc.vector.tensor_tensor(sg3[t][:, c], a_ps[t][:, c], sg3[t][:, c], MULT)

        def finish(adder, t, c=whole):
            adder.tensor_tensor(res[t][:, c], sg2[t][:, c], sg3[t][:, c], ADD)
            nc.sync.dma_start(out_rows[t][:, c], res[t][:, c])

        for t in range(2):
            nc.gpsimd.tensor_tensor(sg2[t][:], b_win[t][:, :S], sg2[t][:], MULT)
        for t in range(2):
            gate_a(t)
            nc.vector.scalar_tensor_tensor(sg2[t + 2][:], b_ps[t + 2][:], 0.0625, sg2[t + 2][:], MULT, MULT)
        gate_a(2)
        for t in range(3):
            finish(nc.gpsimd, t)
        for c in halves:
            gate_a(3, c)
        for c in halves:
            finish(nc.vector, 3, c)
